import numpy as np
import ml_dtypes


def mxq(x, axis, fmt="e4m3"):
    dtype, down = {"e4m3": (ml_dtypes.float8_e4m3fn, 7), "e5m2": (ml_dtypes.float8_e5m2, 14)}[fmt]
    v = np.moveaxis(np.asarray(x, np.float32).astype(ml_dtypes.bfloat16).astype(np.float64), axis, -1)
    blocks = v.reshape(v.shape[:-1] + (-1, 32))
    amax = np.abs(blocks).max(-1, keepdims=True)
    byte = np.maximum(np.where(amax > 0, np.frexp(amax)[1] - 1 + 127, 0) - down, 1)
    scale = np.exp2(byte - 127.0)
    codes = (blocks / scale).astype(np.float32).astype(dtype).astype(np.float64)
    return np.moveaxis((codes * scale).reshape(v.shape), -1, axis)


WIDE = False


def mx_kscale(k):
    if not WIDE:
        return np.ones(k)
    levels = np.array([10, -10, 5, -5, 0])
    if k % 512:
        return np.exp2(np.random.permutation(np.resize(levels, k // 32))).repeat(32)
    a = np.empty((k // 512, 16))
    for p in range(k // 512):
        a[p, :8] = np.random.permutation(np.resize(levels, 8))
        for g in range(8):
            far = levels[np.abs(levels - a[p, g]) >= 10]
            a[p, g + 8] = far[np.random.randint(len(far))]
    return np.exp2(a.ravel()).repeat(32)


def f64(x):
    return np.asarray(x).astype(np.float64)


def striped(idx):
    return np.tile(idx.reshape(-1, 16).T, (8, 1)).astype(np.uint16)


def unstriped(offs):
    return offs[:16].T.reshape(-1).astype(np.int64)


def striped8(idx):
    return np.concatenate([x.reshape(-1, 16).T for x in idx]).astype(np.uint16)


def runs(offs, k):
    lists = np.stack([offs[16 * r : 16 * r + 16].T.reshape(-1) for r in range(8)]).astype(np.int64)
    return lists[np.arange(k) % 512 // 64]


def pack_weight(w):
    k, n = w.shape
    w = f64(np.asarray(w, np.float32).astype(ml_dtypes.bfloat16)).reshape(k // 32, 32, n)
    amax = np.abs(w).max(1)
    byte = np.clip(np.where(amax > 0, np.frexp(amax)[1] - 1 + 127 - 7, 1), 1, 254)
    scaled = (w * np.exp2(127.0 - byte)[:, None, :]).reshape(k, n).astype(np.float32)
    words = np.ascontiguousarray(scaled.reshape(k // 512, 128, 4, n).transpose(0, 1, 3, 2)).astype(ml_dtypes.float8_e4m3fn).view(np.uint8)
    return words, np.ascontiguousarray(byte.astype(np.uint8).reshape(k // 512, 16, n))


def unpack_weight(words, scales):
    g, p, n, _ = words.shape
    vals = np.ascontiguousarray(words).view(ml_dtypes.float8_e4m3fn).astype(np.float64) * np.repeat(np.exp2(scales.astype(np.float64) - 127.0), 8, axis=1)[..., None]
    return vals.transpose(0, 1, 3, 2).reshape(g * 512, n)


K, T, S, N, G, H = 512, 2048, 512, 512, 2048, 512


def setup_inputs():
    n = np.random.standard_normal
    s = mx_kscale(K)[:, None]
    u = mx_kscale(H)
    packed_xT = pack_weight(n((K, T)) * s)
    packed_dT = pack_weight(n((K, G)) / s)
    return {
        "x_words": packed_xT[0],
        "x_scales": packed_xT[1],
        "d_words": packed_dT[0],
        "d_scales": packed_dT[1],
        "gn": (np.random.uniform(0.5, 1.5, (H, 1)) * u[:, None]).astype(np.float32),
        "w1": (n((H, N)) / np.sqrt(H) / u[:, None]).astype(np.float32),
        "offs": striped(np.random.permutation(T)[:S]),
        "kidx": striped8(np.random.randint(0, G, (8, H))),
    }


def reference(x_words, x_scales, d_words, d_scales, gn, w1, offs, kidx):
    d_kidx = unpack_weight(d_words, d_scales)[np.arange(K)[:, None], runs(kidx, K)]
    xq = unpack_weight(x_words, x_scales)[:, unstriped(offs)]
    s = 0.03125 * (d_kidx.T @ xq)
    e = np.exp(s - s.max(axis=1, keepdims=True))
    p = e / e.sum(axis=1, keepdims=True)
    z = f64(gn) * (64.0 * p)
    return mxq(f64(w1), 0, "e4m3").T @ mxq(z, 0, "e4m3")

@@ -1,0 +1,193 @@
+from contextlib import ExitStack
+
+import concourse.mybir as mybir
+
+K, T, S, N, G, H = 512, 2048, 512, 512, 2048, 512
+FLOPS = 2 * K * H * S + 2 * H * N * S
+
+F32 = mybir.dt.float32
+BF16 = mybir.dt.bfloat16
+I32 = mybir.dt.int32
+U32 = mybir.dt.uint32
+U16 = mybir.dt.uint16
+U8 = mybir.dt.uint8
+FP8X4 = mybir.dt.float8_e4m3fn_x4
+ALU = mybir.AluOpType
+ACT = mybir.ActivationFunctionType
+
+P = 128
+PACK = 4
+HALF = S // 2
+W_SCALAR = 256
+
+
+def tile_picked_coattn_none_p_kernel(
+    tc, x_words, x_scales, d_words, d_scales, gn, w1, offs, kidx, out
+):
+    nc = tc.nc
+    with ExitStack() as ctx:
+        sb = ctx.enter_context(tc.tile_pool(name="sb", bufs=1))
+        ps = ctx.enter_context(tc.psum_pool(name="ps", bufs=1))
+
+        kidx_t = sb.tile([P, H // 16], U16, name="kidx_t")
+        offs_t = sb.tile([P, S // 16], U16, name="offs_t")
+        d_scale_win = sb.tile([P, G], U8, name="d_scale_win", align_bytes=64)
+        x_scale_win = sb.tile([P, T], U8, name="x_scale_win", align_bytes=64)
+        d_word_win = sb.tile([P, G], I32, name="d_word_win", align_bytes=64)
+        x_word_win = sb.tile([P, T], I32, name="x_word_win", align_bytes=64)
+        w_raw = sb.tile([P, PACK, N], F32, name="w_raw", align_bytes=64)
+        gn_t = sb.tile([P, PACK], F32, name="gn_t")
+
+        nc.gpsimd.memset(d_scale_win[:].bitcast(I32), 0)
+        nc.vector.memset(x_scale_win[:].bitcast(I32), 0)
+
+        nc.sync.dma_start(kidx_t[:], kidx)
+        nc.sync.dma_start(offs_t[:], offs)
+        nc.sync.dma_start(gn_t[:], gn.rearrange("(p t) o -> p (t o)", t=PACK))
+        nc.sync.dma_start(d_scale_win[0:P:8, :].bitcast(I32), d_scales[0].bitcast(I32))
+        nc.sync.dma_start(x_scale_win[0:P:8, :].bitcast(I32), x_scales[0].bitcast(I32))
+        nc.sync.dma_start(d_word_win[:], d_words[0].rearrange("p n t -> p (n t)").bitcast(I32))
+        nc.sync.dma_start(x_word_win[:], x_words[0].rearrange("p n t -> p (n t)").bitcast(I32))
+        nc.sync.dma_start(w_raw[:], w1.rearrange("(p j) m -> p j m", j=PACK))
+
+        warm = sb.tile([P, 1], F32, name="warm")
+        nc.scalar.activation(warm[:], gn_t[:, 0:1], ACT.Exp, scale=0.0)
+        gain = sb.tile([P, PACK], F32, name="gain")
+        nc.gpsimd.tensor_scalar(gain[:], gn_t[:], 64.0, 0.0, ALU.mult, ALU.add)
+
+        d_scale_picked = sb.tile([P, H], U8, name="d_scale_picked", align_bytes=64)
+        x_scale_picked = sb.tile([P, S], U8, name="x_scale_picked", align_bytes=64)
+        planes = sb.tile([P, H + S], U8, name="planes", align_bytes=64)
+        nc.vector.tensor_copy(d_scale_picked[:], d_scale_win[:].indirect(kidx_t[:]))
+        nc.vector.tensor_copy(
+            planes[:, 0:H].rearrange("p (t m) -> p t m", t=PACK),
+            d_scale_picked[:].rearrange("p (m t) -> p t m", t=PACK),
+        )
+        nc.vector.tensor_copy(x_scale_picked[:], x_scale_win[:].indirect(offs_t[:]))
+        nc.vector.tensor_copy(planes[:, H : H + S].bitcast(I32), x_scale_picked[:].bitcast(I32))
+        for u in range(1, 4):
+            nc.scalar.dma_start(planes[u:P:32, :].bitcast(I32), planes[8 * u : P : 32, :].bitcast(I32))
+
+        d_picked = sb.tile([P, H], U32, name="d_picked", align_bytes=64)
+        d_codes = sb.tile([P, H], U32, name="d_codes", align_bytes=64)
+        x_codes = sb.tile([P, S], U32, name="x_codes", align_bytes=64)
+        nc.vector.tensor_copy(d_picked[:], d_word_win[:].bitcast(U32).indirect(kidx_t[:]))
+        nc.vector.tensor_copy(
+            d_codes[:].bitcast(I32).rearrange("p (t m) -> p m t", t=PACK),
+            d_picked[:].bitcast(I32).rearrange("p (m t) -> p m t", t=PACK),
+        )
+        nc.vector.tensor_copy(x_codes[:], x_word_win[:].bitcast(U32).indirect(offs_t[:]))
+
+        w_bf = sb.tile([P, N, PACK], BF16, name="w_bf", align_bytes=64)
+        nc.scalar.copy(
+            w_bf[:, 0:W_SCALAR, :].rearrange("p (c i) j -> p c j i", i=4),
+            w_raw[:, :, 0:W_SCALAR].rearrange("p j (c i) -> p c j i", i=4),
+        )
+        nc.gpsimd.tensor_scalar(
+            w_bf[:, W_SCALAR:N, :].rearrange("p (c i) j -> p c j i", i=4),
+            w_raw[:, :, W_SCALAR:N].rearrange("p j (c i) -> p c j i", i=4),
+            1.0, 0.0, ALU.mult, ALU.add,
+        )
+
+        neg_s = [sb.tile([P, S], F32, name="neg_s%d" % t) for t in range(PACK)]
+        e = [sb.tile([P, S], F32, name="e%d" % t) for t in range(PACK)]
+        neg_max = sb.tile([P, PACK], F32, name="neg_max")
+        total = sb.tile([P, PACK], F32, name="total")
+        inv = sb.tile([P, PACK], F32, name="inv")
+        factor = sb.tile([P, PACK], F32, name="factor")
+        z_rows = [sb.tile([P, PACK, HALF], BF16, name="z_rows%d" % h, align_bytes=64) for h in range(2)]
+        w_codes = sb.tile([P, N], U32, name="w_codes", align_bytes=64)
+        w_plane = sb.tile([P, N], U8, name="w_plane", align_bytes=64)
+        z_bf = [sb.tile([P, HALF, PACK], BF16, name="z_bf%d" % h, align_bytes=64) for h in range(2)]
+        z_codes = [sb.tile([P, HALF], U32, name="z_codes%d" % h, align_bytes=64) for h in range(2)]
+        z_plane = [sb.tile([P, HALF], U8, name="z_plane%d" % h, align_bytes=64) for h in range(2)]
+
+        def invert(t):
+            nc.vector.reciprocal(inv[:, t : t + 1], total[:, t : t + 1])
+
+        def scale_first(t):
+            nc.vector.tensor_scalar(
+                z_rows[0][:, t, :], e[t][:, 0:HALF], inv[:, t : t + 1], gain[:, t : t + 1], ALU.mult, ALU.mult
+            )
+
+        def join(lo, hi):
+            nc.vector.tensor_tensor(factor[:, lo:hi], inv[:, lo:hi], gain[:, lo:hi], ALU.mult)
+
+        def scale_second(t):
+            nc.scalar.activation(z_rows[1][:, t, :], e[t][:, HALF:S], ACT.Copy, scale=factor[:, t : t + 1])
+
+        def quantize_w(b):
+            cols = slice(b * (N // 2), (b + 1) * (N // 2))
+            nc.vector.quantize_mx(
+                w_codes[:, cols].bitcast(FP8X4), w_plane[:, cols], w_bf[:, cols, :].rearrange("p m j -> p (m j)")
+            )
+
+        def weave(h, copy):
+            copy(
+                z_bf[h][:].rearrange("p (c i) t -> p c t i", i=4),
+                z_rows[h][:].rearrange("p t (c i) -> p c t i", i=4),
+            )
+
+        def quantize_z(h):
+            nc.vector.quantize_mx(
+                z_codes[h][:].bitcast(FP8X4), z_plane[h][:], z_bf[h][:].rearrange("p j t -> p (j t)")
+            )
+
+        for t in range(PACK):
+            cols = slice(t * P, (t + 1) * P)
+            score = ps.tile([P, S], F32, name="score%d" % t)
+            nc.tensor.matmul_mx(
+                score[:], lhsT=d_codes[:, cols].bitcast(FP8X4), lhsT_scale=planes[:, cols],
+                rhs=x_codes[:].bitcast(FP8X4), rhs_scale=planes[:, H : H + S], start=True, stop=True,
+            )
+            if t == 3:
+                invert(0)
+            nc.vector.tensor_scalar(
+                neg_s[t][:], score[:], -0.03125, None, ALU.mult, ALU.min, accum_out=neg_max[:, t : t + 1]
+            )
+            nc.scalar.activation(
+                e[t][:], neg_s[t][:], ACT.Exp, bias=neg_max[:, t : t + 1], scale=-1.0,
+                accum_out=total[:, t : t + 1],
+            )
+        invert(1)
+        scale_first(0)
+        invert(2)
+        scale_first(1)
+        join(0, 3)
+        scale_first(2)
+        invert(3)
+        for t in range(3):
+            scale_second(t)
+        quantize_w(0)
+        scale_first(3)
+        join(3, 4)
+        scale_second(3)
+        weave(0, nc.vector.tensor_copy)
+        weave(1, nc.scalar.copy)
+        quantize_w(1)
+        quantize_z(0)
+        quantize_z(1)
+
+        out_rows = out.rearrange("(a p) j -> p a j", p=P)
+        drain = [nc.scalar.copy, nc.vector.tensor_copy]
+
+        def product(acc, m, h):
+            cols = slice(m * P, (m + 1) * P)
+            nc.tensor.matmul_mx(
+                acc, lhsT=w_codes[:, cols].bitcast(FP8X4), lhsT_scale=w_plane[:, cols],
+                rhs=z_codes[h][:].bitcast(FP8X4), rhs_scale=z_plane[h][:], start=True, stop=True,
+            )
+
+        for b in range(2):
+            acc = ps.tile([P, 2, HALF], F32, name="acc%d" % b)
+            for a in range(2):
+                product(acc[:, a, :], 2 * b + a, 0)
+            staged = sb.tile([P, 2, HALF], F32, name="staged%d" % b)
+            drain[b](staged[:], acc[:])
+            nc.sync.dma_start(out_rows[:, 2 * b : 2 * b + 2, 0:HALF], staged[:])
+        for m in range(PACK):
+            last = ps.tile([P, S], F32, name="score%d" % m)
+            product(last[:, 0:HALF], m, 1)
+            staged = sb.tile([P, HALF], F32, name="staged_last%d" % m)
+            drain[m % 2](staged[:], last[:, 0:HALF])
+            nc.sync.dma_start(out_rows[:, m, HALF:S], staged[:])

@@ -18,7 +18,6 @@ ACT = mybir.ActivationFunctionType
 P = 128
 PACK = 4
 HALF = S // 2
-W_SCALAR = 256
 
 
 def tile_picked_coattn_none_p_kernel(
@@ -34,68 +33,71 @@ def tile_picked_coattn_none_p_kernel(
         d_scale_win = sb.tile([P, G], U8, name="d_scale_win", align_bytes=64)
         x_scale_win = sb.tile([P, T], U8, name="x_scale_win", align_bytes=64)
         d_word_win = sb.tile([P, G], I32, name="d_word_win", align_bytes=64)
-        x_word_win = sb.tile([P, T], I32, name="x_word_win", align_bytes=64)
-        w_raw = sb.tile([P, PACK, N], F32, name="w_raw", align_bytes=64)
+        x_word_win = sb.tile([P, T], I32, name="x_word_win", tag="x_table", align_bytes=64)
+        w_raw0 = sb.tile([P, PACK, N // 2], F32, name="w_raw0", tag="w_first", align_bytes=64)
         gn_t = sb.tile([P, PACK], F32, name="gn_t")
+        w_rows = w1.rearrange("(p j) m -> p j m", j=PACK)
 
-        nc.gpsimd.memset(d_scale_win[:].bitcast(I32), 0)
+        nc.vector.memset(d_scale_win[:].bitcast(I32), 0)
         nc.vector.memset(x_scale_win[:].bitcast(I32), 0)
 
         nc.sync.dma_start(kidx_t[:], kidx)
         nc.sync.dma_start(offs_t[:], offs)
-        nc.sync.dma_start(gn_t[:], gn.rearrange("(p t) o -> p (t o)", t=PACK))
         nc.sync.dma_start(d_scale_win[0:P:8, :].bitcast(I32), d_scales[0].bitcast(I32))
         nc.sync.dma_start(x_scale_win[0:P:8, :].bitcast(I32), x_scales[0].bitcast(I32))
         nc.sync.dma_start(d_word_win[:], d_words[0].rearrange("p n t -> p (n t)").bitcast(I32))
         nc.sync.dma_start(x_word_win[:], x_words[0].rearrange("p n t -> p (n t)").bitcast(I32))
-        nc.sync.dma_start(w_raw[:], w1.rearrange("(p j) m -> p j m", j=PACK))
+        nc.sync.dma_start(w_raw0[:], w_rows[:, :, 0 : N // 2])
+        nc.sync.dma_start(gn_t[:], gn.rearrange("(p t) o -> p (t o)", t=PACK))
 
-        warm = sb.tile([P, 1], F32, name="warm")
-        nc.scalar.activation(warm[:], gn_t[:, 0:1], ACT.Exp, scale=0.0)
         gain = sb.tile([P, PACK], F32, name="gain")
-        nc.gpsimd.tensor_scalar(gain[:], gn_t[:], 64.0, 0.0, ALU.mult, ALU.add)
+        nc.scalar.activation(gain[:], gn_t[:], ACT.Copy, scale=64.0)
 
         d_scale_picked = sb.tile([P, H], U8, name="d_scale_picked", align_bytes=64)
-        x_scale_picked = sb.tile([P, S], U8, name="x_scale_picked", align_bytes=64)
+        x_scale_picked = sb.tile([P, S], U8, name="x_scale_picked", tag="relay", align_bytes=64)
         planes = sb.tile([P, H + S], U8, name="planes", align_bytes=64)
         nc.vector.tensor_copy(d_scale_picked[:], d_scale_win[:].indirect(kidx_t[:]))
+        nc.vector.tensor_copy(x_scale_picked[:], x_scale_win[:].indirect(offs_t[:]))
         nc.vector.tensor_copy(
             planes[:, 0:H].rearrange("p (t m) -> p t m", t=PACK),
             d_scale_picked[:].rearrange("p (m t) -> p t m", t=PACK),
         )
-        nc.vector.tensor_copy(x_scale_picked[:], x_scale_win[:].indirect(offs_t[:]))
         nc.vector.tensor_copy(planes[:, H : H + S].bitcast(I32), x_scale_picked[:].bitcast(I32))
         for u in range(1, 4):
-            nc.scalar.dma_start(planes[u:P:32, :].bitcast(I32), planes[8 * u : P : 32, :].bitcast(I32))
+            nc.sync.dma_start(planes[u:P:32, :].bitcast(I32), planes[8 * u : P : 32, :].bitcast(I32))
+        w_raw1 = sb.tile([P, PACK, N // 2], F32, name="w_raw1", tag="relay", align_bytes=64)
+        nc.sync.dma_start(w_raw1[:], w_rows[:, :, N // 2 : N])
 
         d_picked = sb.tile([P, H], U32, name="d_picked", align_bytes=64)
-        d_codes = sb.tile([P, H], U32, name="d_codes", align_bytes=64)
+        d_first = sb.tile([P, P], U32, name="d_first", align_bytes=64)
         x_codes = sb.tile([P, S], U32, name="x_codes", align_bytes=64)
         nc.vector.tensor_copy(d_picked[:], d_word_win[:].bitcast(U32).indirect(kidx_t[:]))
+        dealt = d_picked[:].bitcast(I32).rearrange("p (m t) -> p m t", t=PACK)
+        nc.vector.tensor_copy(d_first[:].bitcast(I32), dealt[:, :, 0])
+        for h in range(2):
+            nc.vector.tensor_copy(
+                x_codes[:, h * HALF : (h + 1) * HALF],
+                x_word_win[:].bitcast(U32).indirect(offs_t[:, h * (HALF // 16) : (h + 1) * (HALF // 16)]),
+            )
+        d_rest = sb.tile([P, H - P], U32, name="d_rest", tag="x_table", align_bytes=64)
         nc.vector.tensor_copy(
-            d_codes[:].bitcast(I32).rearrange("p (t m) -> p m t", t=PACK),
-            d_picked[:].bitcast(I32).rearrange("p (m t) -> p m t", t=PACK),
+            d_rest[:].bitcast(I32).rearrange("p (t m) -> p m t", t=PACK - 1), dealt[:, :, 1:PACK]
         )
-        nc.vector.tensor_copy(x_codes[:], x_word_win[:].bitcast(U32).indirect(offs_t[:]))
+        d_codes = [d_first[:]] + [d_rest[:, t * P : (t + 1) * P] for t in range(PACK - 1)]
 
-        w_bf = sb.tile([P, N, PACK], BF16, name="w_bf", align_bytes=64)
-        nc.scalar.copy(
-            w_bf[:, 0:W_SCALAR, :].rearrange("p (c i) j -> p c j i", i=4),
-            w_raw[:, :, 0:W_SCALAR].rearrange("p j (c i) -> p c j i", i=4),
-        )
-        nc.gpsimd.tensor_scalar(
-            w_bf[:, W_SCALAR:N, :].rearrange("p (c i) j -> p c j i", i=4),
-            w_raw[:, :, W_SCALAR:N].rearrange("p j (c i) -> p c j i", i=4),
-            1.0, 0.0, ALU.mult, ALU.add,
-        )
+        def weave(copy, dst, src):
+            copy(dst.rearrange("p (c i) t -> p c t i", i=4), src.rearrange("p t (c i) -> p c t i", i=4))
 
-        neg_s = [sb.tile([P, S], F32, name="neg_s%d" % t) for t in range(PACK)]
-        e = [sb.tile([P, S], F32, name="e%d" % t) for t in range(PACK)]
+        w_bf0 = sb.tile([P, N // 2, PACK], BF16, name="w_bf0", align_bytes=64)
+        weave(nc.scalar.copy, w_bf0[:], w_raw0[:])
+
+        neg_s = [sb.tile([P, S], F32, name="neg_s%d" % t, align_bytes=64) for t in range(PACK)]
+        e = [sb.tile([P, S], F32, name="e0", tag="w_first", align_bytes=64)]
+        e = e + [sb.tile([P, S], F32, name="e%d" % t) for t in range(1, PACK)]
         neg_max = sb.tile([P, PACK], F32, name="neg_max")
         total = sb.tile([P, PACK], F32, name="total")
         inv = sb.tile([P, PACK], F32, name="inv")
-        factor = sb.tile([P, PACK], F32, name="factor")
-        z_rows = [sb.tile([P, PACK, HALF], BF16, name="z_rows%d" % h, align_bytes=64) for h in range(2)]
+        z_rows = sb.tile([P, PACK, S], BF16, name="z_rows", align_bytes=64)
         w_codes = sb.tile([P, N], U32, name="w_codes", align_bytes=64)
         w_plane = sb.tile([P, N], U8, name="w_plane", align_bytes=64)
         z_bf = [sb.tile([P, HALF, PACK], BF16, name="z_bf%d" % h, align_bytes=64) for h in range(2)]
@@ -105,28 +107,14 @@ def tile_picked_coattn_none_p_kernel(
         def invert(t):
             nc.vector.reciprocal(inv[:, t : t + 1], total[:, t : t + 1])
 
-        def scale_first(t):
+        def normalise(t, lo, hi):
             nc.vector.tensor_scalar(
-                z_rows[0][:, t, :], e[t][:, 0:HALF], inv[:, t : t + 1], gain[:, t : t + 1], ALU.mult, ALU.mult
+                z_rows[:, t, lo:hi], e[t][:, lo:hi], inv[:, t : t + 1], gain[:, t : t + 1], ALU.mult, ALU.mult
             )
 
-        def join(lo, hi):
-            nc.vector.tensor_tensor(factor[:, lo:hi], inv[:, lo:hi], gain[:, lo:hi], ALU.mult)
-
-        def scale_second(t):
-            nc.scalar.activation(z_rows[1][:, t, :], e[t][:, HALF:S], ACT.Copy, scale=factor[:, t : t + 1])
-
-        def quantize_w(b):
+        def quantize_w(b, src):
             cols = slice(b * (N // 2), (b + 1) * (N // 2))
-            nc.vector.quantize_mx(
-                w_codes[:, cols].bitcast(FP8X4), w_plane[:, cols], w_bf[:, cols, :].rearrange("p m j -> p (m j)")
-            )
-
-        def weave(h, copy):
-            copy(
-                z_bf[h][:].rearrange("p (c i) t -> p c t i", i=4),
-                z_rows[h][:].rearrange("p t (c i) -> p c t i", i=4),
-            )
+            nc.vector.quantize_mx(w_codes[:, cols].bitcast(FP8X4), w_plane[:, cols], src.rearrange("p m j -> p (m j)"))
 
         def quantize_z(h):
             nc.vector.quantize_mx(
@@ -136,10 +124,13 @@ def tile_picked_coattn_none_p_kernel(
         for t in range(PACK):
             cols = slice(t * P, (t + 1) * P)
             score = ps.tile([P, S], F32, name="score%d" % t)
-            nc.tensor.matmul_mx(
-                score[:], lhsT=d_codes[:, cols].bitcast(FP8X4), lhsT_scale=planes[:, cols],
-                rhs=x_codes[:].bitcast(FP8X4), rhs_scale=planes[:, H : H + S], start=True, stop=True,
-            )
+            width = HALF if t == 0 else S
+            for lo in range(0, S, width):
+                nc.tensor.matmul_mx(
+                    score[:, lo : lo + width], lhsT=d_codes[t].bitcast(FP8X4), lhsT_scale=planes[:, cols],
+                    rhs=x_codes[:, lo : lo + width].bitcast(FP8X4), rhs_scale=planes[:, H + lo : H + lo + width],
+                    start=True, stop=True,
+                )
             if t == 3:
                 invert(0)
             nc.vector.tensor_scalar(
@@ -149,45 +140,33 @@ def tile_picked_coattn_none_p_kernel(
                 e[t][:], neg_s[t][:], ACT.Exp, bias=neg_max[:, t : t + 1], scale=-1.0,
                 accum_out=total[:, t : t + 1],
             )
+        w_bf1 = sb.tile([P, N // 2, PACK], BF16, name="w_bf1", tag="neg_s3", align_bytes=64)
+        weave(nc.scalar.copy, w_bf1[:], w_raw1[:])
         invert(1)
-        scale_first(0)
+        normalise(0, 0, S)
         invert(2)
-        scale_first(1)
-        join(0, 3)
-        scale_first(2)
+        normalise(1, 0, S)
+        normalise(2, 0, S)
         invert(3)
-        for t in range(3):
-            scale_second(t)
-        quantize_w(0)
-        scale_first(3)
-        join(3, 4)
-        scale_second(3)
-        weave(0, nc.vector.tensor_copy)
-        weave(1, nc.scalar.copy)
-        quantize_w(1)
+        quantize_w(0, w_bf0[:])
+        normalise(3, 0, S)
+        weave(nc.vector.tensor_copy, z_bf[0][:], z_rows[:, :, 0:HALF])
+        weave(nc.scalar.copy, z_bf[1][:], z_rows[:, :, HALF:S])
         quantize_z(0)
+        quantize_w(1, w_bf1[:])
         quantize_z(1)
 
         out_rows = out.rearrange("(a p) j -> p a j", p=P)
-        drain = [nc.scalar.copy, nc.vector.tensor_copy]
-
-        def product(acc, m, h):
-            cols = slice(m * P, (m + 1) * P)
-            nc.tensor.matmul_mx(
-                acc, lhsT=w_codes[:, cols].bitcast(FP8X4), lhsT_scale=w_plane[:, cols],
-                rhs=z_codes[h][:].bitcast(FP8X4), rhs_scale=z_plane[h][:], start=True, stop=True,
-            )
-
-        for b in range(2):
-            acc = ps.tile([P, 2, HALF], F32, name="acc%d" % b)
-            for a in range(2):
-                product(acc[:, a, :], 2 * b + a, 0)
-            staged = sb.tile([P, 2, HALF], F32, name="staged%d" % b)
-            drain[b](staged[:], acc[:])
-            nc.sync.dma_start(out_rows[:, 2 * b : 2 * b + 2, 0:HALF], staged[:])
-        for m in range(PACK):
-            last = ps.tile([P, S], F32, name="score%d" % m)
-            product(last[:, 0:HALF], m, 1)
-            staged = sb.tile([P, HALF], F32, name="staged_last%d" % m)
-            drain[m % 2](staged[:], last[:, 0:HALF])
-            nc.sync.dma_start(out_rows[:, m, HALF:S], staged[:])
+        drain = [[nc.scalar.copy, nc.scalar.copy, nc.vector.tensor_copy, nc.scalar.copy],
+                 [nc.vector.tensor_copy, nc.scalar.copy, nc.vector.tensor_copy, nc.scalar.copy]]
+        for h in range(2):
+            for m in range(PACK):
+                cols = slice(m * P, (m + 1) * P)
+                acc = ps.tile([P, S], F32, name=["acc%d", "score%d"][h] % m)
+                nc.tensor.matmul_mx(
+                    acc[:, 0:HALF], lhsT=w_codes[:, cols].bitcast(FP8X4), lhsT_scale=w_plane[:, cols],
+                    rhs=z_codes[h][:].bitcast(FP8X4), rhs_scale=z_plane[h][:], start=True, stop=True,
+                )
+                staged = sb.tile([P, HALF], F32, name="staged%d%d" % (h, m))
+                drain[h][m](staged[:], acc[:, 0:HALF])
+                nc.sync.dma_start(out_rows[:, m, h * HALF : (h + 1) * HALF], staged[:])

@@ -18,6 +18,7 @@ ACT = mybir.ActivationFunctionType
 P = 128
 PACK = 4
 HALF = S // 2
+QUARTER = S // 4
 
 
 def tile_picked_coattn_none_p_kernel(
@@ -100,9 +101,9 @@ def tile_picked_coattn_none_p_kernel(
         z_rows = sb.tile([P, PACK, S], BF16, name="z_rows", align_bytes=64)
         w_codes = sb.tile([P, N], U32, name="w_codes", align_bytes=64)
         w_plane = sb.tile([P, N], U8, name="w_plane", align_bytes=64)
-        z_bf = [sb.tile([P, HALF, PACK], BF16, name="z_bf%d" % h, align_bytes=64) for h in range(2)]
-        z_codes = [sb.tile([P, HALF], U32, name="z_codes%d" % h, align_bytes=64) for h in range(2)]
-        z_plane = [sb.tile([P, HALF], U8, name="z_plane%d" % h, align_bytes=64) for h in range(2)]
+        z_bf = sb.tile([P, S, PACK], BF16, name="z_bf", align_bytes=64)
+        z_codes = sb.tile([P, S], U32, name="z_codes", align_bytes=64)
+        z_plane = sb.tile([P, S], U8, name="z_plane", align_bytes=64)
 
         def invert(t):
             nc.vector.reciprocal(inv[:, t : t + 1], total[:, t : t + 1])
@@ -116,9 +117,9 @@ def tile_picked_coattn_none_p_kernel(
             cols = slice(b * (N // 2), (b + 1) * (N // 2))
             nc.vector.quantize_mx(w_codes[:, cols].bitcast(FP8X4), w_plane[:, cols], src.rearrange("p m j -> p (m j)"))
 
-        def quantize_z(h):
+        def quantize_z(lo, hi):
             nc.vector.quantize_mx(
-                z_codes[h][:].bitcast(FP8X4), z_plane[h][:], z_bf[h][:].rearrange("p j t -> p (j t)")
+                z_codes[:, lo:hi].bitcast(FP8X4), z_plane[:, lo:hi], z_bf[:, lo:hi, :].rearrange("p j t -> p (j t)")
             )
 
         for t in range(PACK):
@@ -136,9 +137,15 @@ def tile_picked_coattn_none_p_kernel(
             nc.vector.tensor_scalar(
                 neg_s[t][:], score[:], -0.03125, None, ALU.mult, ALU.min, accum_out=neg_max[:, t : t + 1]
             )
+            source, scale = (neg_s[t], -1.0) if t < 3 else (score, 0.03125)
             nc.scalar.activation(
-                e[t][:], neg_s[t][:], ACT.Exp, bias=neg_max[:, t : t + 1], scale=-1.0,
+                e[t][:], source[:], ACT.Exp, bias=neg_max[:, t : t + 1], scale=scale,
                 accum_out=total[:, t : t + 1],
+            )
+        for n in range(2):
+            nc.tensor.matmul_mx(
+                score[:], lhsT=d_codes[3].bitcast(FP8X4), lhsT_scale=planes[:, cols],
+                rhs=x_codes[:].bitcast(FP8X4), rhs_scale=planes[:, H : H + S], start=True, stop=True,
             )
         w_bf1 = sb.tile([P, N // 2, PACK], BF16, name="w_bf1", tag="neg_s3", align_bytes=64)
         weave(nc.scalar.copy, w_bf1[:], w_raw1[:])
@@ -149,24 +156,30 @@ def tile_picked_coattn_none_p_kernel(
         normalise(2, 0, S)
         invert(3)
         quantize_w(0, w_bf0[:])
-        normalise(3, 0, S)
-        weave(nc.vector.tensor_copy, z_bf[0][:], z_rows[:, :, 0:HALF])
-        weave(nc.scalar.copy, z_bf[1][:], z_rows[:, :, HALF:S])
-        quantize_z(0)
+        normalise(3, 0, QUARTER)
+        normalise(3, QUARTER, S)
+        for q in range(2):
+            cols = slice(q * QUARTER, (q + 1) * QUARTER)
+            weave(nc.vector.tensor_copy, z_bf[:, cols, :], z_rows[:, :, cols])
+        weave(nc.scalar.copy, z_bf[:, HALF:S, :], z_rows[:, :, HALF:S])
+        quantize_z(0, QUARTER)
+        quantize_z(QUARTER, HALF)
         quantize_w(1, w_bf1[:])
-        quantize_z(1)
+        quantize_z(HALF, S)
 
         out_rows = out.rearrange("(a p) j -> p a j", p=P)
-        drain = [[nc.scalar.copy, nc.scalar.copy, nc.vector.tensor_copy, nc.scalar.copy],
-                 [nc.vector.tensor_copy, nc.scalar.copy, nc.vector.tensor_copy, nc.scalar.copy]]
-        for h in range(2):
-            for m in range(PACK):
+        pieces = [(0, 2, 0, QUARTER), (0, 2, QUARTER, HALF), (2, 3, 0, HALF), (3, 4, 0, HALF)]
+        pieces = pieces + [(m, m + 1, HALF, S) for m in range(PACK)]
+        drain = [nc.scalar.copy] * 3 + [nc.vector.tensor_copy, nc.scalar.copy] * 2 + [nc.vector.tensor_copy]
+        banks = ["acc%d" % b for b in range(4)] + ["score%d" % b for b in range(4)]
+        for n, (m0, m1, lo, hi) in enumerate(pieces):
+            acc = ps.tile([P, m1 - m0, hi - lo], F32, name=banks[n])
+            for m in range(m0, m1):
                 cols = slice(m * P, (m + 1) * P)
-                acc = ps.tile([P, S], F32, name=["acc%d", "score%d"][h] % m)
                 nc.tensor.matmul_mx(
-                    acc[:, 0:HALF], lhsT=w_codes[:, cols].bitcast(FP8X4), lhsT_scale=w_plane[:, cols],
-                    rhs=z_codes[h][:].bitcast(FP8X4), rhs_scale=z_plane[h][:], start=True, stop=True,
+                    acc[:, m - m0, :], lhsT=w_codes[:, cols].bitcast(FP8X4), lhsT_scale=w_plane[:, cols],
+                    rhs=z_codes[:, lo:hi].bitcast(FP8X4), rhs_scale=z_plane[:, lo:hi], start=True, stop=True,
                 )
-                staged = sb.tile([P, HALF], F32, name="staged%d%d" % (h, m))
-                drain[h][m](staged[:], acc[:, 0:HALF])
-                nc.sync.dma_start(out_rows[:, m, h * HALF : (h + 1) * HALF], staged[:])
+            staged = sb.tile([P, m1 - m0, hi - lo], F32, name="staged%d" % n)
+            drain[n](staged[:], acc[:])
+            nc.sync.dma_start(out_rows[:, m0:m1, lo:hi], staged[:])

@@ -19,6 +19,8 @@ P = 128
 PACK = 4
 HALF = S // 2
 QUARTER = S // 4
+SPLIT_TILES = 2
+W_HALF_BYTES = PACK * (N // 2) * 4
 
 
 def tile_picked_coattn_none_p_kernel(
@@ -27,6 +29,9 @@ def tile_picked_coattn_none_p_kernel(
     nc = tc.nc
     with ExitStack() as ctx:
         sb = ctx.enter_context(tc.tile_pool(name="sb", bufs=1))
+        relay = ctx.enter_context(tc.tile_pool(name="relay", bufs=1))
+        reuse = ctx.enter_context(tc.tile_pool(name="reuse", bufs=1))
+        late = ctx.enter_context(tc.tile_pool(name="late", bufs=1))
         ps = ctx.enter_context(tc.psum_pool(name="ps", bufs=1))
 
         kidx_t = sb.tile([P, H // 16], U16, name="kidx_t")
@@ -34,9 +39,7 @@ def tile_picked_coattn_none_p_kernel(
         d_scale_win = sb.tile([P, G], U8, name="d_scale_win", align_bytes=64)
         x_scale_win = sb.tile([P, T], U8, name="x_scale_win", align_bytes=64)
         d_word_win = sb.tile([P, G], I32, name="d_word_win", align_bytes=64)
-        x_word_win = sb.tile([P, T], I32, name="x_word_win", tag="x_table", align_bytes=64)
-        w_raw0 = sb.tile([P, PACK, N // 2], F32, name="w_raw0", tag="w_first", align_bytes=64)
-        gn_t = sb.tile([P, PACK], F32, name="gn_t")
+        x_word_win = reuse.tile([P, T], I32, name="x_word_win", offset=0, align_bytes=64)
         w_rows = w1.rearrange("(p j) m -> p j m", j=PACK)
 
         nc.vector.memset(d_scale_win[:].bitcast(I32), 0)
@@ -45,17 +48,14 @@ def tile_picked_coattn_none_p_kernel(
         nc.sync.dma_start(kidx_t[:], kidx)
         nc.sync.dma_start(offs_t[:], offs)
         nc.sync.dma_start(d_scale_win[0:P:8, :].bitcast(I32), d_scales[0].bitcast(I32))
+        d_table = d_words[0].rearrange("p n t -> p (n t)").bitcast(I32)
+        nc.sync.dma_start(d_word_win[:, 0 : G // 2], d_table[:, 0 : G // 2])
         nc.sync.dma_start(x_scale_win[0:P:8, :].bitcast(I32), x_scales[0].bitcast(I32))
-        nc.sync.dma_start(d_word_win[:], d_words[0].rearrange("p n t -> p (n t)").bitcast(I32))
+        nc.sync.dma_start(d_word_win[:, G // 2 : G], d_table[:, G // 2 : G])
         nc.sync.dma_start(x_word_win[:], x_words[0].rearrange("p n t -> p (n t)").bitcast(I32))
-        nc.sync.dma_start(w_raw0[:], w_rows[:, :, 0 : N // 2])
-        nc.sync.dma_start(gn_t[:], gn.rearrange("(p t) o -> p (t o)", t=PACK))
-
-        gain = sb.tile([P, PACK], F32, name="gain")
-        nc.scalar.activation(gain[:], gn_t[:], ACT.Copy, scale=64.0)
 
         d_scale_picked = sb.tile([P, H], U8, name="d_scale_picked", align_bytes=64)
-        x_scale_picked = sb.tile([P, S], U8, name="x_scale_picked", tag="relay", align_bytes=64)
+        x_scale_picked = relay.tile([P, S], U8, name="x_scale_picked", offset=W_HALF_BYTES - S // 2, align_bytes=64)
         planes = sb.tile([P, H + S], U8, name="planes", align_bytes=64)
         nc.vector.tensor_copy(d_scale_picked[:], d_scale_win[:].indirect(kidx_t[:]))
         nc.vector.tensor_copy(x_scale_picked[:], x_scale_win[:].indirect(offs_t[:]))
@@ -66,120 +66,150 @@ def tile_picked_coattn_none_p_kernel(
         nc.vector.tensor_copy(planes[:, H : H + S].bitcast(I32), x_scale_picked[:].bitcast(I32))
         for u in range(1, 4):
             nc.sync.dma_start(planes[u:P:32, :].bitcast(I32), planes[8 * u : P : 32, :].bitcast(I32))
-        w_raw1 = sb.tile([P, PACK, N // 2], F32, name="w_raw1", tag="relay", align_bytes=64)
+        w_raw0 = relay.tile([P, PACK, N // 2], F32, name="w_raw0", offset=0, align_bytes=64)
+        w_raw1 = relay.tile([P, PACK, N // 2], F32, name="w_raw1", offset=W_HALF_BYTES + 64, align_bytes=64)
+        nc.sync.dma_start(w_raw0[:], w_rows[:, :, 0 : N // 2])
         nc.sync.dma_start(w_raw1[:], w_rows[:, :, N // 2 : N])
+        gn_t = relay.tile([P, PACK], F32, name="gn_t", offset=W_HALF_BYTES, align_bytes=64)
+        nc.sync.dma_start(gn_t[:], gn.rearrange("(p t) o -> p (t o)", t=PACK))
 
         d_picked = sb.tile([P, H], U32, name="d_picked", align_bytes=64)
-        d_first = sb.tile([P, P], U32, name="d_first", align_bytes=64)
+        d_dealt = sb.tile([P, PACK, P], U32, name="d_dealt", align_bytes=64)
         x_codes = sb.tile([P, S], U32, name="x_codes", align_bytes=64)
-        nc.vector.tensor_copy(d_picked[:], d_word_win[:].bitcast(U32).indirect(kidx_t[:]))
-        dealt = d_picked[:].bitcast(I32).rearrange("p (m t) -> p m t", t=PACK)
-        nc.vector.tensor_copy(d_first[:].bitcast(I32), dealt[:, :, 0])
-        for h in range(2):
+
+        def gather_queries(h):
             nc.vector.tensor_copy(
                 x_codes[:, h * HALF : (h + 1) * HALF],
                 x_word_win[:].bitcast(U32).indirect(offs_t[:, h * (HALF // 16) : (h + 1) * (HALF // 16)]),
             )
-        d_rest = sb.tile([P, H - P], U32, name="d_rest", tag="x_table", align_bytes=64)
-        nc.vector.tensor_copy(
-            d_rest[:].bitcast(I32).rearrange("p (t m) -> p m t", t=PACK - 1), dealt[:, :, 1:PACK]
-        )
-        d_codes = [d_first[:]] + [d_rest[:, t * P : (t + 1) * P] for t in range(PACK - 1)]
+
+        for h in range(2):
+            nc.vector.tensor_copy(
+                d_picked[:, h * (H // 2) : (h + 1) * (H // 2)],
+                d_word_win[:].bitcast(U32).indirect(kidx_t[:, h * (H // 32) : (h + 1) * (H // 32)]),
+            )
+        for h in range(2):
+            nc.vector.tensor_copy(
+                d_dealt[:, :, h * (P // 2) : (h + 1) * (P // 2)].bitcast(I32).rearrange("p t m -> p m t"),
+                d_picked[:, h * (H // 2) : (h + 1) * (H // 2)].bitcast(I32).rearrange("p (m t) -> p m t", t=PACK),
+            )
+        gather_queries(0)
+        gather_queries(1)
+        d_codes = [d_dealt[:, t, :] for t in range(PACK)]
 
         def weave(copy, dst, src):
             copy(dst.rearrange("p (c i) t -> p c t i", i=4), src.rearrange("p t (c i) -> p c t i", i=4))
 
-        w_bf0 = sb.tile([P, N // 2, PACK], BF16, name="w_bf0", align_bytes=64)
-        weave(nc.scalar.copy, w_bf0[:], w_raw0[:])
+        def gpsimd_round(dst, src):
+            nc.gpsimd.tensor_scalar(dst, src, 1.0, 0.0, ALU.mult, ALU.add)
 
-        neg_s = [sb.tile([P, S], F32, name="neg_s%d" % t, align_bytes=64) for t in range(PACK)]
-        e = [sb.tile([P, S], F32, name="e0", tag="w_first", align_bytes=64)]
-        e = e + [sb.tile([P, S], F32, name="e%d" % t) for t in range(1, PACK)]
+        w_bf0 = reuse.tile([P, N // 2, PACK], BF16, name="w_bf0", offset=0, align_bytes=64)
+        w_bf1 = reuse.tile([P, N // 2, PACK], BF16, name="w_bf1", offset=2048, align_bytes=64)
+        weave(gpsimd_round, w_bf0[:], w_raw0[:])
+        weave(gpsimd_round, w_bf1[:], w_raw1[:])
+
+        neg_s = [sb.tile([P, S], F32, name="neg_s%d" % t, align_bytes=64) for t in range(PACK - 1)]
+        neg_s = neg_s + [late.tile([P, S], F32, name="neg_s3", offset=0, align_bytes=64)]
+        e = [sb.tile([P, S], F32, name="e%d" % t) for t in range(PACK)]
+        neg_part = sb.tile([P, SPLIT_TILES], F32, name="neg_part")
         neg_max = sb.tile([P, PACK], F32, name="neg_max")
         total = sb.tile([P, PACK], F32, name="total")
         inv = sb.tile([P, PACK], F32, name="inv")
-        z_rows = sb.tile([P, PACK, S], BF16, name="z_rows", align_bytes=64)
-        w_codes = sb.tile([P, N], U32, name="w_codes", align_bytes=64)
-        w_plane = sb.tile([P, N], U8, name="w_plane", align_bytes=64)
-        z_bf = sb.tile([P, S, PACK], BF16, name="z_bf", align_bytes=64)
-        z_codes = sb.tile([P, S], U32, name="z_codes", align_bytes=64)
+        factor = sb.tile([P, PACK], F32, name="factor")
+        w_plane = [sb.tile([P, N // 2], U8, name="w_plane%d" % b, align_bytes=64) for b in range(2)]
         z_plane = sb.tile([P, S], U8, name="z_plane", align_bytes=64)
 
-        def invert(t):
-            nc.vector.reciprocal(inv[:, t : t + 1], total[:, t : t + 1])
+        def invert(lo, hi):
+            nc.vector.reciprocal(inv[:, lo:hi], total[:, lo:hi])
 
-        def normalise(t, lo, hi):
-            nc.vector.tensor_scalar(
-                z_rows[:, t, lo:hi], e[t][:, lo:hi], inv[:, t : t + 1], gain[:, t : t + 1], ALU.mult, ALU.mult
+        def normalise(dst, t, lo, hi):
+            nc.vector.tensor_scalar(dst, e[t][:, lo:hi], inv[:, t : t + 1], gain[:, t : t + 1], ALU.mult, ALU.mult)
+
+        def normalise_on_scalar(dst, t, lo, hi):
+            nc.scalar.activation(dst, e[t][:, lo:hi], ACT.Copy, scale=factor[:, t : t + 1])
+
+        def quantize(codes, plane, woven):
+            nc.vector.quantize_mx(codes.bitcast(FP8X4), plane, woven.rearrange("p c t -> p (c t)"))
+
+        def scores(bank, t, lo, hi):
+            score = ps.tile([P, hi - lo], F32, name=bank)
+            nc.tensor.matmul_mx(
+                score[:], lhsT=d_codes[t].bitcast(FP8X4), lhsT_scale=planes[:, t * P : (t + 1) * P],
+                rhs=x_codes[:, lo:hi].bitcast(FP8X4), rhs_scale=planes[:, H + lo : H + hi], start=True, stop=True,
             )
+            return score
 
-        def quantize_w(b, src):
-            cols = slice(b * (N // 2), (b + 1) * (N // 2))
-            nc.vector.quantize_mx(w_codes[:, cols].bitcast(FP8X4), w_plane[:, cols], src.rearrange("p m j -> p (m j)"))
+        def negated_max(t, lo, hi, score, start, result):
+            nc.vector.tensor_scalar(neg_s[t][:, lo:hi], score[:], -0.03125, start, ALU.mult, ALU.min, accum_out=result)
 
-        def quantize_z(lo, hi):
-            nc.vector.quantize_mx(
-                z_codes[:, lo:hi].bitcast(FP8X4), z_plane[:, lo:hi], z_bf[:, lo:hi, :].rearrange("p j t -> p (j t)")
-            )
-
+        for t in range(SPLIT_TILES):
+            negated_max(t, 0, HALF, scores("bank%d" % t, t, 0, HALF), None, neg_part[:, t : t + 1])
         for t in range(PACK):
-            cols = slice(t * P, (t + 1) * P)
-            score = ps.tile([P, S], F32, name="score%d" % t)
-            width = HALF if t == 0 else S
-            for lo in range(0, S, width):
-                nc.tensor.matmul_mx(
-                    score[:, lo : lo + width], lhsT=d_codes[t].bitcast(FP8X4), lhsT_scale=planes[:, cols],
-                    rhs=x_codes[:, lo : lo + width].bitcast(FP8X4), rhs_scale=planes[:, H + lo : H + lo + width],
-                    start=True, stop=True,
-                )
-            if t == 3:
-                invert(0)
-            nc.vector.tensor_scalar(
-                neg_s[t][:], score[:], -0.03125, None, ALU.mult, ALU.min, accum_out=neg_max[:, t : t + 1]
-            )
-            source, scale = (neg_s[t], -1.0) if t < 3 else (score, 0.03125)
+            lo = HALF if t < SPLIT_TILES else 0
+            score = scores("bank%d" % (t + SPLIT_TILES), t, lo, S)
+            negated_max(t, lo, S, score, neg_part[:, t : t + 1] if t < SPLIT_TILES else None, neg_max[:, t : t + 1])
             nc.scalar.activation(
-                e[t][:], source[:], ACT.Exp, bias=neg_max[:, t : t + 1], scale=scale,
+                e[t][:], neg_s[t][:], ACT.Exp, bias=neg_max[:, t : t + 1], scale=-1.0,
                 accum_out=total[:, t : t + 1],
             )
-        for n in range(2):
-            nc.tensor.matmul_mx(
-                score[:], lhsT=d_codes[3].bitcast(FP8X4), lhsT_scale=planes[:, cols],
-                rhs=x_codes[:].bitcast(FP8X4), rhs_scale=planes[:, H : H + S], start=True, stop=True,
-            )
-        w_bf1 = sb.tile([P, N // 2, PACK], BF16, name="w_bf1", tag="neg_s3", align_bytes=64)
-        weave(nc.scalar.copy, w_bf1[:], w_raw1[:])
-        invert(1)
-        normalise(0, 0, S)
-        invert(2)
-        normalise(1, 0, S)
-        normalise(2, 0, S)
-        invert(3)
-        quantize_w(0, w_bf0[:])
-        normalise(3, 0, QUARTER)
-        normalise(3, QUARTER, S)
+        w_codes = [late.tile([P, N // 2], U32, name="w_codes0", offset=0, align_bytes=64)]
+        woven0 = late.tile([P, QUARTER, PACK], BF16, name="woven0", offset=2048, align_bytes=64)
+        woven1 = sb.tile([P, QUARTER, PACK], BF16, name="woven1", align_bytes=64)
+        rows = sb.tile([P, PACK, S - QUARTER], BF16, name="rows", align_bytes=64)
+        codes0 = sb.tile([P, QUARTER], U32, name="codes0", align_bytes=64)
+        codes2 = sb.tile([P, HALF], U32, name="codes2", align_bytes=64)
+
+        invert(0, 2)
+        gain = sb.tile([P, PACK], F32, name="gain")
+        nc.vector.tensor_scalar(gain[:], gn_t[:], 64.0, None, ALU.mult)
+        normalise(woven0[:, :, 0], 0, 0, QUARTER)
+        nc.vector.tensor_tensor(factor[:, 0:2], inv[:, 0:2], gain[:, 0:2], ALU.mult)
+        normalise(woven0[:, :, 1], 1, 0, QUARTER)
+        for t in range(2):
+            normalise_on_scalar(rows[:, t, :], t, QUARTER, S)
+        invert(2, 4)
+        quantize(w_codes[0][:], w_plane[0][:], w_bf0[:])
+        for t in range(2, 4):
+            normalise(woven0[:, :, t], t, 0, QUARTER)
+        nc.vector.tensor_tensor(factor[:, 2:4], inv[:, 2:4], gain[:, 2:4], ALU.mult)
+        for t in range(2, 4):
+            normalise(rows[:, t, 0:QUARTER], t, QUARTER, HALF)
+        for t in range(2, 4):
+            normalise_on_scalar(rows[:, t, QUARTER:], t, HALF, S)
+        quantize(codes0[:], z_plane[:, 0:QUARTER], woven0[:])
+        weave(nc.vector.tensor_copy, woven1[:], rows[:, :, 0:QUARTER])
+        w_codes.append(late.tile([P, N // 2], U32, name="w_codes1", offset=2048, align_bytes=64))
+        quantize(w_codes[1][:], w_plane[1][:], w_bf1[:])
+        codes1 = reuse.tile([P, QUARTER], U32, name="codes1", offset=2048, align_bytes=64)
+        woven2 = reuse.tile([P, HALF, PACK], BF16, name="woven2", offset=3072, align_bytes=64)
+        quantize(codes1[:], z_plane[:, QUARTER:HALF], woven1[:])
         for q in range(2):
             cols = slice(q * QUARTER, (q + 1) * QUARTER)
-            weave(nc.vector.tensor_copy, z_bf[:, cols, :], z_rows[:, :, cols])
-        weave(nc.scalar.copy, z_bf[:, HALF:S, :], z_rows[:, :, HALF:S])
-        quantize_z(0, QUARTER)
-        quantize_z(QUARTER, HALF)
-        quantize_w(1, w_bf1[:])
-        quantize_z(HALF, S)
+            weave(nc.vector.tensor_copy, woven2[:, cols, :], rows[:, :, (q + 1) * QUARTER : (q + 2) * QUARTER])
+        for q in range(2):
+            cols = slice(q * QUARTER, (q + 1) * QUARTER)
+            quantize(codes2[:, cols], z_plane[:, HALF + q * QUARTER : HALF + (q + 1) * QUARTER], woven2[:, cols, :])
 
         out_rows = out.rearrange("(a p) j -> p a j", p=P)
-        pieces = [(0, 2, 0, QUARTER), (0, 2, QUARTER, HALF), (2, 3, 0, HALF), (3, 4, 0, HALF)]
-        pieces = pieces + [(m, m + 1, HALF, S) for m in range(PACK)]
-        drain = [nc.scalar.copy] * 3 + [nc.vector.tensor_copy, nc.scalar.copy] * 2 + [nc.vector.tensor_copy]
-        banks = ["acc%d" % b for b in range(4)] + ["score%d" % b for b in range(4)]
-        for n, (m0, m1, lo, hi) in enumerate(pieces):
-            acc = ps.tile([P, m1 - m0, hi - lo], F32, name=banks[n])
-            for m in range(m0, m1):
-                cols = slice(m * P, (m + 1) * P)
-                nc.tensor.matmul_mx(
-                    acc[:, m - m0, :], lhsT=w_codes[:, cols].bitcast(FP8X4), lhsT_scale=w_plane[:, cols],
-                    rhs=z_codes[:, lo:hi].bitcast(FP8X4), rhs_scale=z_plane[:, lo:hi], start=True, stop=True,
-                )
+        banks = ["bank%d" % ((PACK + SPLIT_TILES + b) % 8) for b in range(8)]
+
+        def product(acc, m, codes, lo):
+            cols = slice((m % 2) * P, (m % 2 + 1) * P)
+            nc.tensor.matmul_mx(
+                acc, lhsT=w_codes[m // 2][:, cols].bitcast(FP8X4), lhsT_scale=w_plane[m // 2][:, cols],
+                rhs=codes.bitcast(FP8X4), rhs_scale=z_plane[:, lo : lo + QUARTER], start=True, stop=True,
+            )
+
+        def store(n, copy, acc, m0, m1, lo, hi):
             staged = sb.tile([P, m1 - m0, hi - lo], F32, name="staged%d" % n)
-            drain[n](staged[:], acc[:])
+            copy(staged[:], acc[:])
             nc.sync.dma_start(out_rows[:, m0:m1, lo:hi], staged[:])
+
+        codes = [codes0[:], codes1[:], codes2[:, 0:QUARTER], codes2[:, QUARTER:HALF]]
+        drain = [nc.scalar.copy] * 4 + [nc.vector.tensor_copy, nc.scalar.copy] * 2
+        for n in range(8):
+            q, m0 = n // 2, 2 * (n % 2)
+            acc = ps.tile([P, 2, QUARTER], F32, name=banks[n])
+            for m in range(2):
+                product(acc[:, m, :], m0 + m, codes[q], q * QUARTER)
+            store(n, drain[n], acc, m0, m0 + 2, q * QUARTER, (q + 1) * QUARTER)

@@ -101,12 +101,12 @@ def tile_picked_coattn_none_p_kernel(
             copy(dst.rearrange("p (c i) t -> p c t i", i=4), src.rearrange("p t (c i) -> p c t i", i=4))
 
         def gpsimd_round(dst, src):
-            nc.gpsimd.tensor_scalar(dst, src, 1.0, 0.0, ALU.mult, ALU.add)
+            nc.gpsimd.tensor_scalar(dst, src.rearrange("p t c -> p c t"), 1.0, 0.0, ALU.mult, ALU.add)
 
         w_bf0 = reuse.tile([P, N // 2, PACK], BF16, name="w_bf0", offset=0, align_bytes=64)
         w_bf1 = reuse.tile([P, N // 2, PACK], BF16, name="w_bf1", offset=2048, align_bytes=64)
-        weave(gpsimd_round, w_bf0[:], w_raw0[:])
-        weave(gpsimd_round, w_bf1[:], w_raw1[:])
+        gpsimd_round(w_bf0[:], w_raw0[:])
+        gpsimd_round(w_bf1[:], w_raw1[:])
 
         neg_s = [sb.tile([P, S], F32, name="neg_s%d" % t, align_bytes=64) for t in range(PACK - 1)]
         neg_s = neg_s + [late.tile([P, S], F32, name="neg_s3", offset=0, align_bytes=64)]

@@ -55,7 +55,7 @@ def tile_picked_coattn_none_p_kernel(
         nc.sync.dma_start(x_word_win[:], x_words[0].rearrange("p n t -> p (n t)").bitcast(I32))
 
         d_scale_picked = sb.tile([P, H], U8, name="d_scale_picked", align_bytes=64)
-        x_scale_picked = relay.tile([P, S], U8, name="x_scale_picked", offset=W_HALF_BYTES - S // 2, align_bytes=64)
+        x_scale_picked = relay.tile([P, S], U8, name="x_scale_picked", offset=2 * W_HALF_BYTES - S // 2, align_bytes=64)
         planes = sb.tile([P, H + S], U8, name="planes", align_bytes=64)
         nc.vector.tensor_copy(d_scale_picked[:], d_scale_win[:].indirect(kidx_t[:]))
         nc.vector.tensor_copy(x_scale_picked[:], x_scale_win[:].indirect(offs_t[:]))
@@ -66,11 +66,10 @@ def tile_picked_coattn_none_p_kernel(
         nc.vector.tensor_copy(planes[:, H : H + S].bitcast(I32), x_scale_picked[:].bitcast(I32))
         for u in range(1, 4):
             nc.sync.dma_start(planes[u:P:32, :].bitcast(I32), planes[8 * u : P : 32, :].bitcast(I32))
-        w_raw0 = relay.tile([P, PACK, N // 2], F32, name="w_raw0", offset=0, align_bytes=64)
-        w_raw1 = relay.tile([P, PACK, N // 2], F32, name="w_raw1", offset=W_HALF_BYTES + 64, align_bytes=64)
-        nc.sync.dma_start(w_raw0[:], w_rows[:, :, 0 : N // 2])
-        nc.sync.dma_start(w_raw1[:], w_rows[:, :, N // 2 : N])
-        gn_t = relay.tile([P, PACK], F32, name="gn_t", offset=W_HALF_BYTES, align_bytes=64)
+        w_raw = relay.tile([P, PACK, PACK, N // 4], F32, name="w_raw", offset=0, align_bytes=64)
+        for q in (2, 0, 1, 3):
+            nc.sync.dma_start(w_raw[:, q, :, :], w_rows[:, :, q * (N // 4) : (q + 1) * (N // 4)])
+        gn_t = relay.tile([P, PACK], F32, name="gn_t", offset=2 * W_HALF_BYTES, align_bytes=64)
         nc.sync.dma_start(gn_t[:], gn.rearrange("(p t) o -> p (t o)", t=PACK))
 
         d_picked = sb.tile([P, H], U32, name="d_picked", align_bytes=64)
@@ -101,12 +100,14 @@ def tile_picked_coattn_none_p_kernel(
             copy(dst.rearrange("p (c i) t -> p c t i", i=4), src.rearrange("p t (c i) -> p c t i", i=4))
 
         def gpsimd_round(dst, src):
-            nc.gpsimd.tensor_scalar(dst, src.rearrange("p t c -> p c t"), 1.0, 0.0, ALU.mult, ALU.add)
+            nc.gpsimd.tensor_scalar(dst, src, 1.0, 0.0, ALU.mult, ALU.add)
 
         w_bf0 = reuse.tile([P, N // 2, PACK], BF16, name="w_bf0", offset=0, align_bytes=64)
-        w_bf1 = reuse.tile([P, N // 2, PACK], BF16, name="w_bf1", offset=2048, align_bytes=64)
-        gpsimd_round(w_bf0[:], w_raw0[:])
-        gpsimd_round(w_bf1[:], w_raw1[:])
+        w_bf1 = late.tile([P, N // 2, PACK], BF16, name="w_bf1", offset=4096, align_bytes=64)
+        weave(lambda dst, src: nc.scalar.activation(dst, src, ACT.Copy), w_bf1[:, 0 : N // 4, :], w_raw[:, 2, :, :])
+        for q in (0, 1, 3):
+            cols = slice((q % 2) * (N // 4), (q % 2 + 1) * (N // 4))
+            weave(gpsimd_round, (w_bf0, w_bf1)[q // 2][:, cols, :], w_raw[:, q, :, :])
 
         neg_s = [sb.tile([P, S], F32, name="neg_s%d" % t, align_bytes=64) for t in range(PACK - 1)]
         neg_s = neg_s + [late.tile([P, S], F32, name="neg_s3", offset=0, align_bytes=64)]
@@ -180,8 +181,8 @@ def tile_picked_coattn_none_p_kernel(
         weave(nc.vector.tensor_copy, woven1[:], rows[:, :, 0:QUARTER])
         w_codes.append(late.tile([P, N // 2], U32, name="w_codes1", offset=2048, align_bytes=64))
         quantize(w_codes[1][:], w_plane[1][:], w_bf1[:])
-        codes1 = reuse.tile([P, QUARTER], U32, name="codes1", offset=2048, align_bytes=64)
-        woven2 = reuse.tile([P, HALF, PACK], BF16, name="woven2", offset=3072, align_bytes=64)
+        codes1 = late.tile([P, QUARTER], U32, name="codes1", offset=4096, align_bytes=64)
+        woven2 = late.tile([P, HALF, PACK], BF16, name="woven2", offset=5120, align_bytes=64)
         quantize(codes1[:], z_plane[:, QUARTER:HALF], woven1[:])
         for q in range(2):
             cols = slice(q * QUARTER, (q + 1) * QUARTER)

@@ -67,7 +67,7 @@ def tile_picked_coattn_none_p_kernel(
         for u in range(1, 4):
             nc.sync.dma_start(planes[u:P:32, :].bitcast(I32), planes[8 * u : P : 32, :].bitcast(I32))
         w_raw = relay.tile([P, PACK, PACK, N // 4], F32, name="w_raw", offset=0, align_bytes=64)
-        for q in (2, 0, 1, 3):
+        for q in (2, 3, 0, 1):
             nc.sync.dma_start(w_raw[:, q, :, :], w_rows[:, :, q * (N // 4) : (q + 1) * (N // 4)])
         gn_t = relay.tile([P, PACK], F32, name="gn_t", offset=2 * W_HALF_BYTES, align_bytes=64)
         nc.sync.dma_start(gn_t[:], gn.rearrange("(p t) o -> p (t o)", t=PACK))
@@ -104,10 +104,10 @@ def tile_picked_coattn_none_p_kernel(
 
         w_bf0 = reuse.tile([P, N // 2, PACK], BF16, name="w_bf0", offset=0, align_bytes=64)
         w_bf1 = late.tile([P, N // 2, PACK], BF16, name="w_bf1", offset=4096, align_bytes=64)
-        weave(lambda dst, src: nc.scalar.activation(dst, src, ACT.Copy), w_bf1[:, 0 : N // 4, :], w_raw[:, 2, :, :])
-        for q in (0, 1, 3):
-            cols = slice((q % 2) * (N // 4), (q % 2 + 1) * (N // 4))
-            weave(gpsimd_round, (w_bf0, w_bf1)[q // 2][:, cols, :], w_raw[:, q, :, :])
+        for q in range(2):
+            cols = slice(q * (N // 4), (q + 1) * (N // 4))
+            weave(lambda dst, src: nc.scalar.activation(dst, src, ACT.Copy), w_bf1[:, cols, :], w_raw[:, 2 + q, :, :])
+            weave(gpsimd_round, w_bf0[:, cols, :], w_raw[:, q, :, :])
 
         neg_s = [sb.tile([P, S], F32, name="neg_s%d" % t, align_bytes=64) for t in range(PACK - 1)]
         neg_s = neg_s + [late.tile([P, S], F32, name="neg_s3", offset=0, align_bytes=64)]

@@ -19,7 +19,10 @@ P = 128
 PACK = 4
 HALF = S // 2
 QUARTER = S // 4
-SPLIT_TILES = 2
+SPLIT_TILES = 3
+QUERY_CUTS = ((0, QUARTER), (QUARTER, S - QUARTER), (S - QUARTER, S))
+WARM_ROWS = 32
+SCALAR_PART = 64
 W_HALF_BYTES = PACK * (N // 2) * 4
 
 
@@ -67,20 +70,15 @@ def tile_picked_coattn_none_p_kernel(
         for u in range(1, 4):
             nc.sync.dma_start(planes[u:P:32, :].bitcast(I32), planes[8 * u : P : 32, :].bitcast(I32))
         w_raw = relay.tile([P, PACK, PACK, N // 4], F32, name="w_raw", offset=0, align_bytes=64)
-        for q in (2, 3, 0, 1):
-            nc.sync.dma_start(w_raw[:, q, :, :], w_rows[:, :, q * (N // 4) : (q + 1) * (N // 4)])
         gn_t = relay.tile([P, PACK], F32, name="gn_t", offset=2 * W_HALF_BYTES, align_bytes=64)
+        for q in range(3):
+            nc.sync.dma_start(w_raw[:, q, :, :], w_rows[:, :, q * P : (q + 1) * P])
         nc.sync.dma_start(gn_t[:], gn.rearrange("(p t) o -> p (t o)", t=PACK))
+        nc.sync.dma_start(w_raw[:, 3, :, :], w_rows[:, :, 3 * P : 4 * P])
 
         d_picked = sb.tile([P, H], U32, name="d_picked", align_bytes=64)
         d_dealt = sb.tile([P, PACK, P], U32, name="d_dealt", align_bytes=64)
         x_codes = sb.tile([P, S], U32, name="x_codes", align_bytes=64)
-
-        def gather_queries(h):
-            nc.vector.tensor_copy(
-                x_codes[:, h * HALF : (h + 1) * HALF],
-                x_word_win[:].bitcast(U32).indirect(offs_t[:, h * (HALF // 16) : (h + 1) * (HALF // 16)]),
-            )
 
         for h in range(2):
             nc.vector.tensor_copy(
@@ -92,8 +90,10 @@ def tile_picked_coattn_none_p_kernel(
                 d_dealt[:, :, h * (P // 2) : (h + 1) * (P // 2)].bitcast(I32).rearrange("p t m -> p m t"),
                 d_picked[:, h * (H // 2) : (h + 1) * (H // 2)].bitcast(I32).rearrange("p (m t) -> p m t", t=PACK),
             )
-        gather_queries(0)
-        gather_queries(1)
+        for lo, hi in QUERY_CUTS:
+            nc.vector.tensor_copy(
+                x_codes[:, lo:hi], x_word_win[:].bitcast(U32).indirect(offs_t[:, lo // 16 : hi // 16])
+            )
         d_codes = [d_dealt[:, t, :] for t in range(PACK)]
 
         def weave(copy, dst, src):
@@ -102,12 +102,15 @@ def tile_picked_coattn_none_p_kernel(
         def gpsimd_round(dst, src):
             nc.gpsimd.tensor_scalar(dst, src, 1.0, 0.0, ALU.mult, ALU.add)
 
-        w_bf0 = reuse.tile([P, N // 2, PACK], BF16, name="w_bf0", offset=0, align_bytes=64)
-        w_bf1 = late.tile([P, N // 2, PACK], BF16, name="w_bf1", offset=4096, align_bytes=64)
-        for q in range(2):
-            cols = slice(q * (N // 4), (q + 1) * (N // 4))
-            weave(lambda dst, src: nc.scalar.activation(dst, src, ACT.Copy), w_bf1[:, cols, :], w_raw[:, 2 + q, :, :])
-            weave(gpsimd_round, w_bf0[:, cols, :], w_raw[:, q, :, :])
+        def scalar_round(dst, src):
+            nc.scalar.activation(dst, src, ACT.Copy)
+
+        w_bf0 = late.tile([P, N // 2, PACK], BF16, name="w_bf0", offset=4096, align_bytes=64)
+        w_bf2 = reuse.tile([P, P, PACK], BF16, name="w_bf2", offset=0, align_bytes=64)
+        weave(scalar_round, w_bf0[:, 0:P, :], w_raw[:, 0, :, :])
+        weave(scalar_round, w_bf0[:, P : P + SCALAR_PART, :], w_raw[:, 1, :, 0:SCALAR_PART])
+        weave(gpsimd_round, w_bf0[:, P + SCALAR_PART : 2 * P, :], w_raw[:, 1, :, SCALAR_PART:P])
+        weave(gpsimd_round, w_bf2[:], w_raw[:, 2, :, :])
 
         neg_s = [sb.tile([P, S], F32, name="neg_s%d" % t, align_bytes=64) for t in range(PACK - 1)]
         neg_s = neg_s + [late.tile([P, S], F32, name="neg_s3", offset=0, align_bytes=64)]
@@ -132,23 +135,29 @@ def tile_picked_coattn_none_p_kernel(
         def quantize(codes, plane, woven):
             nc.vector.quantize_mx(codes.bitcast(FP8X4), plane, woven.rearrange("p c t -> p (c t)"))
 
-        def scores(bank, t, lo, hi):
-            score = ps.tile([P, hi - lo], F32, name=bank)
-            nc.tensor.matmul_mx(
-                score[:], lhsT=d_codes[t].bitcast(FP8X4), lhsT_scale=planes[:, t * P : (t + 1) * P],
-                rhs=x_codes[:, lo:hi].bitcast(FP8X4), rhs_scale=planes[:, H + lo : H + hi], start=True, stop=True,
-            )
+        def scores(bank, t, cuts):
+            first = cuts[0][0]
+            score = ps.tile([P, cuts[-1][1] - first], F32, name=bank)
+            for lo, hi in cuts:
+                nc.tensor.matmul_mx(
+                    score[:, lo - first : hi - first], lhsT=d_codes[t].bitcast(FP8X4),
+                    lhsT_scale=planes[:, t * P : (t + 1) * P], rhs=x_codes[:, lo:hi].bitcast(FP8X4),
+                    rhs_scale=planes[:, H + lo : H + hi], start=True, stop=True,
+                )
             return score
 
         def negated_max(t, lo, hi, score, start, result):
             nc.vector.tensor_scalar(neg_s[t][:, lo:hi], score[:], -0.03125, start, ALU.mult, ALU.min, accum_out=result)
 
         for t in range(SPLIT_TILES):
-            negated_max(t, 0, HALF, scores("bank%d" % t, t, 0, HALF), None, neg_part[:, t : t + 1])
+            negated_max(t, 0, QUARTER, scores("bank%d" % t, t, QUERY_CUTS[:1]), None, neg_part[:, t : t + 1])
         for t in range(PACK):
-            lo = HALF if t < SPLIT_TILES else 0
-            score = scores("bank%d" % (t + SPLIT_TILES), t, lo, S)
-            negated_max(t, lo, S, score, neg_part[:, t : t + 1] if t < SPLIT_TILES else None, neg_max[:, t : t + 1])
+            if t < SPLIT_TILES:
+                score = scores("bank%d" % (t + SPLIT_TILES), t, QUERY_CUTS[1:])
+                negated_max(t, QUARTER, S, score, neg_part[:, t : t + 1], neg_max[:, t : t + 1])
+            else:
+                score = scores("bank%d" % (t + SPLIT_TILES), t, ((0, S),))
+                negated_max(t, 0, S, score, None, neg_max[:, t : t + 1])
             nc.scalar.activation(
                 e[t][:], neg_s[t][:], ACT.Exp, bias=neg_max[:, t : t + 1], scale=-1.0,
                 accum_out=total[:, t : t + 1],
@@ -160,6 +169,16 @@ def tile_picked_coattn_none_p_kernel(
         codes0 = sb.tile([P, QUARTER], U32, name="codes0", align_bytes=64)
         codes2 = sb.tile([P, HALF], U32, name="codes2", align_bytes=64)
 
+        def warm_up(words, plane):
+            unread = ps.tile([WARM_ROWS, H], F32, name="bank6")
+            nc.tensor.matmul_mx(
+                unread[:], lhsT=words[:, 0:WARM_ROWS].bitcast(FP8X4), lhsT_scale=plane[:, 0:WARM_ROWS],
+                rhs=d_dealt[:].rearrange("p t m -> p (t m)").bitcast(FP8X4), rhs_scale=planes[:, 0:H],
+                start=True, stop=True,
+            )
+
+        for t in range(2):
+            warm_up(d_codes[0], planes)
         invert(0, 2)
         gain = sb.tile([P, PACK], F32, name="gain")
         nc.vector.tensor_scalar(gain[:], gn_t[:], 64.0, None, ALU.mult)
@@ -167,9 +186,14 @@ def tile_picked_coattn_none_p_kernel(
         nc.vector.tensor_tensor(factor[:, 0:2], inv[:, 0:2], gain[:, 0:2], ALU.mult)
         normalise(woven0[:, :, 1], 1, 0, QUARTER)
         for t in range(2):
-            normalise_on_scalar(rows[:, t, :], t, QUARTER, S)
+            normalise(rows[:, t, 0:QUARTER], t, QUARTER, HALF)
+        for t in range(2):
+            normalise_on_scalar(rows[:, t, QUARTER:], t, HALF, S)
+        w_bf3 = late.tile([P, P, PACK], BF16, name="w_bf3", offset=1024, align_bytes=64)
+        weave(scalar_round, w_bf3[:], w_raw[:, 3, :, :])
         invert(2, 4)
         quantize(w_codes[0][:], w_plane[0][:], w_bf0[:])
+        warm_up(w_codes[0], w_plane[0])
         for t in range(2, 4):
             normalise(woven0[:, :, t], t, 0, QUARTER)
         nc.vector.tensor_tensor(factor[:, 2:4], inv[:, 2:4], gain[:, 2:4], ALU.mult)
@@ -178,9 +202,10 @@ def tile_picked_coattn_none_p_kernel(
         for t in range(2, 4):
             normalise_on_scalar(rows[:, t, QUARTER:], t, HALF, S)
         quantize(codes0[:], z_plane[:, 0:QUARTER], woven0[:])
-        weave(nc.vector.tensor_copy, woven1[:], rows[:, :, 0:QUARTER])
         w_codes.append(late.tile([P, N // 2], U32, name="w_codes1", offset=2048, align_bytes=64))
-        quantize(w_codes[1][:], w_plane[1][:], w_bf1[:])
+        quantize(w_codes[1][:, 0:P], w_plane[1][:, 0:P], w_bf2[:])
+        weave(nc.vector.tensor_copy, woven1[:], rows[:, :, 0:QUARTER])
+        quantize(w_codes[1][:, P : 2 * P], w_plane[1][:, P : 2 * P], w_bf3[:])
         codes1 = late.tile([P, QUARTER], U32, name="codes1", offset=4096, align_bytes=64)
         woven2 = late.tile([P, HALF, PACK], BF16, name="woven2", offset=5120, align_bytes=64)
         quantize(codes1[:], z_plane[:, QUARTER:HALF], woven1[:])
@@ -192,7 +217,7 @@ def tile_picked_coattn_none_p_kernel(
             quantize(codes2[:, cols], z_plane[:, HALF + q * QUARTER : HALF + (q + 1) * QUARTER], woven2[:, cols, :])
 
         out_rows = out.rearrange("(a p) j -> p a j", p=P)
-        banks = ["bank%d" % ((PACK + SPLIT_TILES + b) % 8) for b in range(8)]
+        banks = ["bank%d" % ((PACK + SPLIT_TILES + b) % 8) for b in range(9)]
 
         def product(acc, m, codes, lo):
             cols = slice((m % 2) * P, (m % 2 + 1) * P)
@@ -207,10 +232,10 @@ def tile_picked_coattn_none_p_kernel(
             nc.sync.dma_start(out_rows[:, m0:m1, lo:hi], staged[:])
 
         codes = [codes0[:], codes1[:], codes2[:, 0:QUARTER], codes2[:, QUARTER:HALF]]
-        drain = [nc.scalar.copy] * 4 + [nc.vector.tensor_copy, nc.scalar.copy] * 2
-        for n in range(8):
-            q, m0 = n // 2, 2 * (n % 2)
-            acc = ps.tile([P, 2, QUARTER], F32, name=banks[n])
-            for m in range(2):
-                product(acc[:, m, :], m0 + m, codes[q], q * QUARTER)
-            store(n, drain[n], acc, m0, m0 + 2, q * QUARTER, (q + 1) * QUARTER)
+        pieces = [(0, 0, 2), (0, 2, 3), (0, 3, 4)] + [(q, m0, m0 + 2) for q in range(1, 4) for m0 in (0, 2)]
+        drain = [nc.scalar.copy] * 5 + [nc.vector.tensor_copy, nc.scalar.copy] * 2
+        for n, (q, m0, m1) in enumerate(pieces):
+            acc = ps.tile([P, m1 - m0, QUARTER], F32, name=banks[n])
+            for m in range(m0, m1):
+                product(acc[:, m - m0, :], m, codes[q], q * QUARTER)
+            store(n, drain[n], acc, m0, m1, q * QUARTER, (q + 1) * QUARTER)

@@ -103,12 +103,12 @@ def tile_picked_coattn_none_p_kernel(
             nc.gpsimd.tensor_scalar(dst, src, 1.0, 0.0, ALU.mult, ALU.add)
 
         def scalar_round(dst, src):
-            nc.scalar.activation(dst, src, ACT.Copy)
+            nc.scalar.activation(dst, src.rearrange("p t c -> p c t"), ACT.Copy)
 
         w_bf0 = late.tile([P, N // 2, PACK], BF16, name="w_bf0", offset=4096, align_bytes=64)
         w_bf2 = reuse.tile([P, P, PACK], BF16, name="w_bf2", offset=0, align_bytes=64)
-        weave(scalar_round, w_bf0[:, 0:P, :], w_raw[:, 0, :, :])
-        weave(scalar_round, w_bf0[:, P : P + SCALAR_PART, :], w_raw[:, 1, :, 0:SCALAR_PART])
+        scalar_round(w_bf0[:, 0:P, :], w_raw[:, 0, :, :])
+        scalar_round(w_bf0[:, P : P + SCALAR_PART, :], w_raw[:, 1, :, 0:SCALAR_PART])
         weave(gpsimd_round, w_bf0[:, P + SCALAR_PART : 2 * P, :], w_raw[:, 1, :, SCALAR_PART:P])
         weave(gpsimd_round, w_bf2[:], w_raw[:, 2, :, :])
 
@@ -190,7 +190,7 @@ def tile_picked_coattn_none_p_kernel(
         for t in range(2):
             normalise_on_scalar(rows[:, t, QUARTER:], t, HALF, S)
         w_bf3 = late.tile([P, P, PACK], BF16, name="w_bf3", offset=1024, align_bytes=64)
-        weave(scalar_round, w_bf3[:], w_raw[:, 3, :, :])
+        scalar_round(w_bf3[:], w_raw[:, 3, :, :])
         invert(2, 4)
         quantize(w_codes[0][:], w_plane[0][:], w_bf0[:])
         warm_up(w_codes[0], w_plane[0])

from contextlib import ExitStack

import concourse.mybir as mybir

K, T, S, N, G, H = 512, 2048, 512, 512, 2048, 512
FLOPS = 2 * K * H * S + 2 * H * N * S

F32 = mybir.dt.float32
BF16 = mybir.dt.bfloat16
I32 = mybir.dt.int32
U32 = mybir.dt.uint32
U16 = mybir.dt.uint16
U8 = mybir.dt.uint8
FP8X4 = mybir.dt.float8_e4m3fn_x4
ALU = mybir.AluOpType
ACT = mybir.ActivationFunctionType

P = 128
PACK = 4
HALF = S // 2
QUARTER = S // 4
SPLIT_TILES = 3
QUERY_CUTS = ((0, QUARTER), (QUARTER, S - QUARTER), (S - QUARTER, S))
WARM_ROWS = 32
SCALAR_PART = 64
W_HALF_BYTES = PACK * (N // 2) * 4


def tile_picked_coattn_none_p_kernel(
    tc, x_words, x_scales, d_words, d_scales, gn, w1, offs, kidx, out
):
    nc = tc.nc
    with ExitStack() as ctx:
        sb = ctx.enter_context(tc.tile_pool(name="sb", bufs=1))
        relay = ctx.enter_context(tc.tile_pool(name="relay", bufs=1))
        reuse = ctx.enter_context(tc.tile_pool(name="reuse", bufs=1))
        late = ctx.enter_context(tc.tile_pool(name="late", bufs=1))
        ps = ctx.enter_context(tc.psum_pool(name="ps", bufs=1))

        kidx_t = sb.tile([P, H // 16], U16, name="kidx_t")
        offs_t = sb.tile([P, S // 16], U16, name="offs_t")
        d_scale_win = sb.tile([P, G], U8, name="d_scale_win", align_bytes=64)
        x_scale_win = sb.tile([P, T], U8, name="x_scale_win", align_bytes=64)
        d_word_win = sb.tile([P, G], I32, name="d_word_win", align_bytes=64)
        x_word_win = reuse.tile([P, T], I32, name="x_word_win", offset=0, align_bytes=64)
        w_rows = w1.rearrange("(p j) m -> p j m", j=PACK)

        nc.vector.memset(d_scale_win[:].bitcast(I32), 0)
        nc.vector.memset(x_scale_win[:].bitcast(I32), 0)

        nc.sync.dma_start(kidx_t[:], kidx)
        nc.sync.dma_start(offs_t[:], offs)
        nc.sync.dma_start(d_scale_win[0:P:8, :].bitcast(I32), d_scales[0].bitcast(I32))
        d_table = d_words[0].rearrange("p n t -> p (n t)").bitcast(I32)
        nc.sync.dma_start(d_word_win[:, 0 : G // 2], d_table[:, 0 : G // 2])
        nc.sync.dma_start(x_scale_win[0:P:8, :].bitcast(I32), x_scales[0].bitcast(I32))
        nc.sync.dma_start(d_word_win[:, G // 2 : G], d_table[:, G // 2 : G])
        nc.sync.dma_start(x_word_win[:], x_words[0].rearrange("p n t -> p (n t)").bitcast(I32))

        d_scale_picked = sb.tile([P, H], U8, name="d_scale_picked", align_bytes=64)
        x_scale_picked = relay.tile([P, S], U8, name="x_scale_picked", offset=2 * W_HALF_BYTES - S // 2, align_bytes=64)
        planes = sb.tile([P, H + S], U8, name="planes", align_bytes=64)
        nc.vector.tensor_copy(d_scale_picked[:], d_scale_win[:].indirect(kidx_t[:]))
        nc.vector.tensor_copy(x_scale_picked[:], x_scale_win[:].indirect(offs_t[:]))
        nc.vector.tensor_copy(
            planes[:, 0:H].rearrange("p (t m) -> p t m", t=PACK),
            d_scale_picked[:].rearrange("p (m t) -> p t m", t=PACK),
        )
        nc.vector.tensor_copy(planes[:, H : H + S].bitcast(I32), x_scale_picked[:].bitcast(I32))
        for u in range(1, 4):
            nc.sync.dma_start(planes[u:P:32, :].bitcast(I32), planes[8 * u : P : 32, :].bitcast(I32))
        w_raw = relay.tile([P, PACK, PACK, N // 4], F32, name="w_raw", offset=0, align_bytes=64)
        gn_t = relay.tile([P, PACK], F32, name="gn_t", offset=2 * W_HALF_BYTES, align_bytes=64)
        for q in range(3):
            nc.sync.dma_start(w_raw[:, q, :, :], w_rows[:, :, q * P : (q + 1) * P])
        nc.sync.dma_start(gn_t[:], gn.rearrange("(p t) o -> p (t o)", t=PACK))
        nc.sync.dma_start(w_raw[:, 3, :, :], w_rows[:, :, 3 * P : 4 * P])

        d_picked = sb.tile([P, H], U32, name="d_picked", align_bytes=64)
        d_dealt = sb.tile([P, PACK, P], U32, name="d_dealt", align_bytes=64)
        x_codes = sb.tile([P, S], U32, name="x_codes", align_bytes=64)

        for h in range(2):
            nc.vector.tensor_copy(
                d_picked[:, h * (H // 2) : (h + 1) * (H // 2)],
                d_word_win[:].bitcast(U32).indirect(kidx_t[:, h * (H // 32) : (h + 1) * (H // 32)]),
            )
        for h in range(2):
            nc.vector.tensor_copy(
                d_dealt[:, :, h * (P // 2) : (h + 1) * (P // 2)].bitcast(I32).rearrange("p t m -> p m t"),
                d_picked[:, h * (H // 2) : (h + 1) * (H // 2)].bitcast(I32).rearrange("p (m t) -> p m t", t=PACK),
            )
        for lo, hi in QUERY_CUTS:
            nc.vector.tensor_copy(
                x_codes[:, lo:hi], x_word_win[:].bitcast(U32).indirect(offs_t[:, lo // 16 : hi // 16])
            )
        d_codes = [d_dealt[:, t, :] for t in range(PACK)]

        def weave(copy, dst, src):
            copy(dst.rearrange("p (c i) t -> p c t i", i=4), src.rearrange("p t (c i) -> p c t i", i=4))

        def gpsimd_round(dst, src):
            nc.gpsimd.tensor_scalar(dst, src, 1.0, 0.0, ALU.mult, ALU.add)

        def scalar_round(dst, src):
            nc.scalar.activation(dst, src.rearrange("p t c -> p c t"), ACT.Copy)

        w_bf0 = late.tile([P, N // 2, PACK], BF16, name="w_bf0", offset=4096, align_bytes=64)
        w_bf2 = reuse.tile([P, P, PACK], BF16, name="w_bf2", offset=0, align_bytes=64)
        scalar_round(w_bf0[:, 0:P, :], w_raw[:, 0, :, :])
        scalar_round(w_bf0[:, P : P + SCALAR_PART, :], w_raw[:, 1, :, 0:SCALAR_PART])
        weave(gpsimd_round, w_bf0[:, P + SCALAR_PART : 2 * P, :], w_raw[:, 1, :, SCALAR_PART:P])
        weave(gpsimd_round, w_bf2[:], w_raw[:, 2, :, :])

        neg_s = [sb.tile([P, S], F32, name="neg_s%d" % t, align_bytes=64) for t in range(PACK - 1)]
        neg_s = neg_s + [late.tile([P, S], F32, name="neg_s3", offset=0, align_bytes=64)]
        e = [sb.tile([P, S], F32, name="e%d" % t) for t in range(PACK)]
        neg_part = sb.tile([P, SPLIT_TILES], F32, name="neg_part")
        neg_max = sb.tile([P, PACK], F32, name="neg_max")
        total = sb.tile([P, PACK], F32, name="total")
        inv = sb.tile([P, PACK], F32, name="inv")
        factor = sb.tile([P, PACK], F32, name="factor")
        w_plane = [sb.tile([P, N // 2], U8, name="w_plane%d" % b, align_bytes=64) for b in range(2)]
        z_plane = sb.tile([P, S], U8, name="z_plane", align_bytes=64)

        def invert(lo, hi):
            nc.vector.reciprocal(inv[:, lo:hi], total[:, lo:hi])

        def normalise(dst, t, lo, hi):
            nc.vector.tensor_scalar(dst, e[t][:, lo:hi], inv[:, t : t + 1], gain[:, t : t + 1], ALU.mult, ALU.mult)

        def normalise_on_scalar(dst, t, lo, hi):
            nc.scalar.activation(dst, e[t][:, lo:hi], ACT.Copy, scale=factor[:, t : t + 1])

        def quantize(codes, plane, woven):
            nc.vector.quantize_mx(codes.bitcast(FP8X4), plane, woven.rearrange("p c t -> p (c t)"))

        def scores(bank, t, cuts):
            first = cuts[0][0]
            score = ps.tile([P, cuts[-1][1] - first], F32, name=bank)
            for lo, hi in cuts:
                nc.tensor.matmul_mx(
                    score[:, lo - first : hi - first], lhsT=d_codes[t].bitcast(FP8X4),
                    lhsT_scale=planes[:, t * P : (t + 1) * P], rhs=x_codes[:, lo:hi].bitcast(FP8X4),
                    rhs_scale=planes[:, H + lo : H + hi], start=True, stop=True,
                )
            return score

        def negated_max(t, lo, hi, score, start, result):
            nc.vector.tensor_scalar(neg_s[t][:, lo:hi], score[:], -0.03125, start, ALU.mult, ALU.min, accum_out=result)

        for t in range(SPLIT_TILES):
            negated_max(t, 0, QUARTER, scores("bank%d" % t, t, QUERY_CUTS[:1]), None, neg_part[:, t : t + 1])
        for t in range(PACK):
            if t < SPLIT_TILES:
                score = scores("bank%d" % (t + SPLIT_TILES), t, QUERY_CUTS[1:])
                negated_max(t, QUARTER, S, score, neg_part[:, t : t + 1], neg_max[:, t : t + 1])
            else:
                score = scores("bank%d" % (t + SPLIT_TILES), t, ((0, S),))
                negated_max(t, 0, S, score, None, neg_max[:, t : t + 1])
            nc.scalar.activation(
                e[t][:], neg_s[t][:], ACT.Exp, bias=neg_max[:, t : t + 1], scale=-1.0,
                accum_out=total[:, t : t + 1],
            )
        w_codes = [late.tile([P, N // 2], U32, name="w_codes0", offset=0, align_bytes=64)]
        woven0 = late.tile([P, QUARTER, PACK], BF16, name="woven0", offset=2048, align_bytes=64)
        woven1 = sb.tile([P, QUARTER, PACK], BF16, name="woven1", align_bytes=64)
        rows = sb.tile([P, PACK, S - QUARTER], BF16, name="rows", align_bytes=64)
        codes0 = sb.tile([P, QUARTER], U32, name="codes0", align_bytes=64)
        codes2 = sb.tile([P, HALF], U32, name="codes2", align_bytes=64)

        def warm_up(words, plane):
            unread = ps.tile([WARM_ROWS, H], F32, name="bank6")
            nc.tensor.matmul_mx(
                unread[:], lhsT=words[:, 0:WARM_ROWS].bitcast(FP8X4), lhsT_scale=plane[:, 0:WARM_ROWS],
                rhs=d_dealt[:].rearrange("p t m -> p (t m)").bitcast(FP8X4), rhs_scale=planes[:, 0:H],
                start=True, stop=True,
            )

        for t in range(2):
            warm_up(d_codes[0], planes)
        invert(0, 2)
        gain = sb.tile([P, PACK], F32, name="gain")
        nc.vector.tensor_scalar(gain[:], gn_t[:], 64.0, None, ALU.mult)
        normalise(woven0[:, :, 0], 0, 0, QUARTER)
        nc.vector.tensor_tensor(factor[:, 0:2], inv[:, 0:2], gain[:, 0:2], ALU.mult)
        normalise(woven0[:, :, 1], 1, 0, QUARTER)
        for t in range(2):
            normalise(rows[:, t, 0:QUARTER], t, QUARTER, HALF)
        for t in range(2):
            normalise_on_scalar(rows[:, t, QUARTER:], t, HALF, S)
        w_bf3 = late.tile([P, P, PACK], BF16, name="w_bf3", offset=1024, align_bytes=64)
        scalar_round(w_bf3[:], w_raw[:, 3, :, :])
        invert(2, 4)
        quantize(w_codes[0][:], w_plane[0][:], w_bf0[:])
        warm_up(w_codes[0], w_plane[0])
        for t in range(2, 4):
            normalise(woven0[:, :, t], t, 0, QUARTER)
        nc.vector.tensor_tensor(factor[:, 2:4], inv[:, 2:4], gain[:, 2:4], ALU.mult)
        for t in range(2, 4):
            normalise(rows[:, t, 0:QUARTER], t, QUARTER, HALF)
        for t in range(2, 4):
            normalise_on_scalar(rows[:, t, QUARTER:], t, HALF, S)
        quantize(codes0[:], z_plane[:, 0:QUARTER], woven0[:])
        w_codes.append(late.tile([P, N // 2], U32, name="w_codes1", offset=2048, align_bytes=64))
        quantize(w_codes[1][:, 0:P], w_plane[1][:, 0:P], w_bf2[:])
        weave(nc.vector.tensor_copy, woven1[:], rows[:, :, 0:QUARTER])
        quantize(w_codes[1][:, P : 2 * P], w_plane[1][:, P : 2 * P], w_bf3[:])
        codes1 = late.tile([P, QUARTER], U32, name="codes1", offset=4096, align_bytes=64)
        woven2 = late.tile([P, HALF, PACK], BF16, name="woven2", offset=5120, align_bytes=64)
        quantize(codes1[:], z_plane[:, QUARTER:HALF], woven1[:])
        for q in range(2):
            cols = slice(q * QUARTER, (q + 1) * QUARTER)
            weave(nc.vector.tensor_copy, woven2[:, cols, :], rows[:, :, (q + 1) * QUARTER : (q + 2) * QUARTER])
        for q in range(2):
            cols = slice(q * QUARTER, (q + 1) * QUARTER)
            quantize(codes2[:, cols], z_plane[:, HALF + q * QUARTER : HALF + (q + 1) * QUARTER], woven2[:, cols, :])

        out_rows = out.rearrange("(a p) j -> p a j", p=P)
        banks = ["bank%d" % ((PACK + SPLIT_TILES + b) % 8) for b in range(9)]

        def product(acc, m, codes, lo):
            cols = slice((m % 2) * P, (m % 2 + 1) * P)
            nc.tensor.matmul_mx(
                acc, lhsT=w_codes[m // 2][:, cols].bitcast(FP8X4), lhsT_scale=w_plane[m // 2][:, cols],
                rhs=codes.bitcast(FP8X4), rhs_scale=z_plane[:, lo : lo + QUARTER], start=True, stop=True,
            )

        def store(n, copy, acc, m0, m1, lo, hi):
            staged = sb.tile([P, m1 - m0, hi - lo], F32, name="staged%d" % n)
            copy(staged[:], acc[:])
            nc.sync.dma_start(out_rows[:, m0:m1, lo:hi], staged[:])

        codes = [codes0[:], codes1[:], codes2[:, 0:QUARTER], codes2[:, QUARTER:HALF]]
        pieces = [(0, 0, 2), (0, 2, 3), (0, 3, 4)] + [(q, m0, m0 + 2) for q in range(1, 4) for m0 in (0, 2)]
        drain = [nc.scalar.copy] * 5 + [nc.vector.tensor_copy, nc.scalar.copy] * 2
        for n, (q, m0, m1) in enumerate(pieces):
            acc = ps.tile([P, m1 - m0, QUARTER], F32, name=banks[n])
            for m in range(m0, m1):
                product(acc[:, m - m0, :], m, codes[q], q * QUARTER)
            store(n, drain[n], acc, m0, m1, q * QUARTER, (q + 1) * QUARTER)
